import numpy as np
import ml_dtypes


def mxq(x, axis, fmt="e4m3"):
    dtype, down = {"e4m3": (ml_dtypes.float8_e4m3fn, 7), "e5m2": (ml_dtypes.float8_e5m2, 14)}[fmt]
    v = np.moveaxis(np.asarray(x, np.float32).astype(ml_dtypes.bfloat16).astype(np.float64), axis, -1)
    blocks = v.reshape(v.shape[:-1] + (-1, 32))
    amax = np.abs(blocks).max(-1, keepdims=True)
    byte = np.maximum(np.where(amax > 0, np.frexp(amax)[1] - 1 + 127, 0) - down, 1)
    scale = np.exp2(byte - 127.0)
    codes = (blocks / scale).astype(np.float32).astype(dtype).astype(np.float64)
    return np.moveaxis((codes * scale).reshape(v.shape), -1, axis)


WIDE = False


def mx_kscale(k):
    if not WIDE:
        return np.ones(k)
    levels = np.array([10, -10, 5, -5, 0])
    if k % 512:
        return np.exp2(np.random.permutation(np.resize(levels, k // 32))).repeat(32)
    a = np.empty((k // 512, 16))
    for p in range(k // 512):
        a[p, :8] = np.random.permutation(np.resize(levels, 8))
        for g in range(8):
            far = levels[np.abs(levels - a[p, g]) >= 10]
            a[p, g + 8] = far[np.random.randint(len(far))]
    return np.exp2(a.ravel()).repeat(32)


def f64(x):
    return np.asarray(x).astype(np.float64)


def striped8(idx):
    return np.asarray(idx).reshape(8, -1, 16).transpose(0, 2, 1).reshape(128, -1).astype(np.uint16)


def unstriped8(offs):
    return offs.reshape(8, 16, -1).transpose(0, 2, 1).reshape(8, -1).astype(np.int64)


def pick8(x, idx, run):
    r = np.arange(len(x))
    return x[r[:, None], idx[r % (8 * run) // run]]


E2M1 = np.array([0.0, 0.5, 1.0, 1.5, 2.0, 3.0, 4.0, 6.0, -0.0, -0.5, -1.0, -1.5, -2.0, -3.0, -4.0, -6.0])


def pack_weight(w, fmt):
    k, n = w.shape
    w = f64(np.asarray(w, np.float32).astype(ml_dtypes.bfloat16)).reshape(k // 32, 32, n)
    amax = np.abs(w).max(1)
    if fmt == "e4m3":
        byte = np.frexp(amax)[1] - 1 + 127 - 7
    else:
        mant, ex = np.frexp(amax / 6.0)
        byte = np.where(mant > 0.5, ex, ex - 1) + 127
    byte = np.clip(np.where(amax > 0, byte, 1), 1, 254)
    scaled = (w * np.exp2(127.0 - byte)[:, None, :]).reshape(k, n).astype(np.float32)
    by_word = np.ascontiguousarray(scaled.reshape(k // 512, 128, 4, n).transpose(0, 1, 3, 2))
    if fmt == "e4m3":
        words = by_word.astype(ml_dtypes.float8_e4m3fn).view(np.uint8)
    else:
        c = by_word.astype(ml_dtypes.float4_e2m1fn).view(np.uint8) & 0xF
        words = (c[..., 0::2] | (c[..., 1::2] << 4)).reshape(k // 512, 128, 2 * n)
    return np.ascontiguousarray(words), np.ascontiguousarray(byte.astype(np.uint8).reshape(k // 512, 16, n))


def unpack_weight(words, scales, fmt):
    g, _, n = scales.shape
    words = np.ascontiguousarray(words).reshape(g, 128, n, -1)
    if fmt == "e4m3":
        vals = words.view(ml_dtypes.float8_e4m3fn).astype(np.float64)
    else:
        nib = np.empty((g, 128, n, 4), np.uint8)
        nib[..., 0::2] = words & 0xF
        nib[..., 1::2] = words >> 4
        vals = E2M1[nib]
    vals = vals * np.repeat(np.exp2(scales.astype(np.float64) - 127.0), 8, axis=1)[..., None]
    return vals.transpose(0, 1, 3, 2).reshape(g * 512, n)


D, T, I, Q = 512, 1024, 512, 128


def setup_inputs():
    n = np.random.standard_normal
    idx = np.stack([np.random.permutation(T)[:I] for _ in range(8)])
    idx2 = np.stack([np.random.permutation(T)[:I] for _ in range(8)])
    idx3 = np.stack([np.random.permutation(T)[:I] for _ in range(8)])
    idx4 = np.stack([np.random.permutation(T)[:I] for _ in range(8)])
    fd = mx_kscale(D)
    keysp = pack_weight(n((D, T)) / fd[:, None], "e4m3")
    return {
        "query": (n((D, Q)) * 0.9 / np.sqrt(D) * fd[:, None]).astype(np.float32),
        "query2": (n((D, Q)) * 0.9 / np.sqrt(D) * fd[:, None]).astype(np.float32),
        "keys_words": keysp[0],
        "keys_scales": keysp[1],
        "lam": (np.random.uniform(1.0, 2.5, (Q, 1))).astype(np.float32),
        "old": (1.0 * n((Q, T))).astype(np.float32),
        "offs": striped8(idx),
        "offs2": striped8(idx2),
        "offs3": striped8(idx3),
        "offs4": striped8(idx4),
    }


def reference(query, query2, keys_words, keys_scales, lam, old, offs, offs2, offs3, offs4):
    idx = unstriped8(offs)
    idx2 = unstriped8(offs2)
    idx3 = unstriped8(offs3)
    idx4 = unstriped8(offs4)
    keysu = unpack_weight(keys_words, keys_scales, "e4m3")
    queryq = mxq(f64(query), 0, "e4m3")
    a = queryq.T @ keysu
    query2q = mxq(f64(query2), 0, "e4m3")
    b = query2q.T @ keysu
    e1s = np.exp(pick8(a, idx, 16))
    w = e1s / (e1s + np.exp(pick8(a, idx2, 16)) + np.exp(pick8(b, idx3, 16))) * f64(lam)
    f1 = np.zeros((Q, T))
    f1[np.arange(Q)[:, None], idx4[np.arange(Q) % 128 // 16]] = w
    y = f64(old) + f1
    return y

@@ -1,0 +1,137 @@
+from contextlib import ExitStack
+
+import concourse.mybir as mybir
+
+D, T, I, Q = 512, 1024, 512, 128
+FLOPS = 2 * 2 * D * T * Q
+
+F32 = mybir.dt.float32
+BF16 = mybir.dt.bfloat16
+I32 = mybir.dt.int32
+U32 = mybir.dt.uint32
+U16 = mybir.dt.uint16
+U8 = mybir.dt.uint8
+FP8X4 = mybir.dt.float8_e4m3fn_x4
+ALU = mybir.AluOpType
+ACT = mybir.ActivationFunctionType
+
+P = 128
+PACK = 4
+HALF_T = T // 2
+HALF_I = I // 2
+PIECE = 128
+STORE = 256
+
+
+def tile_attend_quotaratio_lean_putold_heads_kernel(
+    tc, query, query2, keys_words, keys_scales, lam, old, offs, offs2, offs3, offs4, out
+):
+    nc = tc.nc
+    with ExitStack() as ctx:
+        keep = ctx.enter_context(tc.tile_pool(name="keep", bufs=1))
+        psum = ctx.enter_context(tc.psum_pool(name="psum", bufs=1))
+
+        key_scale = keep.tile([P, T], U8, name="key_scale", align_bytes=64)
+        nc.vector.memset(key_scale[:].bitcast(I32), 0)
+        for g in range(4):
+            nc.scalar.dma_start(
+                out=key_scale[32 * g : 32 * g + 4, :].bitcast(I32),
+                in_=keys_scales[0, 4 * g : 4 * g + 4, :].bitcast(I32),
+            )
+
+        words = keys_words[0].rearrange("p n t -> p (n t)").bitcast(I32)
+        q_raw = [keep.tile([P, PACK, Q], F32, name=f"q_raw{j}") for j in range(2)]
+        key_code = [keep.tile([P, HALF_T], U32, name=f"key_code{h}", align_bytes=64) for h in range(2)]
+        for j, src in enumerate((query, query2)):
+            nc.sync.dma_start(out=q_raw[j][:], in_=src.rearrange("(p t) q -> p t q", t=PACK))
+            nc.sync.dma_start(out=key_code[j][:].bitcast(I32), in_=words[:, j * HALF_T : (j + 1) * HALF_T])
+        lists = []
+        for j, src in enumerate((offs, offs2, offs3, offs4)):
+            tile = keep.tile([P, I // 16], U16, name=f"list{j}")
+            nc.sync.dma_start(tile[:], src)
+            lists.append(tile)
+        lam_col = keep.tile([P, 1], F32, name="lam_col")
+        nc.sync.dma_start(out=lam_col[:], in_=lam)
+        old_sb = keep.tile([P, T], F32, name="old_sb")
+        nc.sync.dma_start(out=old_sb[:], in_=old)
+
+        placed = keep.tile([P, T], F32, name="placed")
+        nc.vector.memset(placed[:], 0.0)
+
+        def quantise(j):
+            grouped = keep.tile([P, Q, PACK], BF16, name=f"grouped{j}", align_bytes=64)
+            nc.vector.tensor_copy(out=grouped[:], in_=q_raw[j][:].rearrange("p t q -> p q t"))
+            code = keep.tile([P, Q], U32, name=f"q_code{j}", align_bytes=64)
+            scale = keep.tile([P, Q], U8, name=f"q_scale{j}", align_bytes=64)
+            nc.vector.quantize_mx(
+                out=code[:].bitcast(FP8X4), scales=scale[:], in_=grouped[:].rearrange("p q t -> p (q t)")
+            )
+            return code, scale
+
+        def score(qq, lo, hi, name):
+            bank = psum.tile([P, hi - lo], F32, name=name)
+            h = lo // HALF_T
+            nc.tensor.matmul_mx(
+                out=bank[:],
+                lhsT=qq[0][:].bitcast(FP8X4),
+                lhsT_scale=qq[1][:],
+                rhs=key_code[h][:, lo - h * HALF_T : hi - h * HALF_T].bitcast(FP8X4),
+                rhs_scale=key_scale[:, lo:hi],
+                start=True,
+                stop=True,
+            )
+            return bank
+
+        a = keep.tile([P, T], F32, name="a")
+        b = keep.tile([P, T], F32, name="b")
+        qa = quantise(0)
+        nc.scalar.copy(a[:, 0:512], score(qa, 0, 512, "a0")[:])
+        qb = quantise(1)
+        nc.scalar.copy(a[:, 512:768], score(qa, 512, 768, "a1")[:])
+        nc.vector.tensor_copy(a[:, 768:1024], score(qa, 768, 1024, "a2")[:])
+        bank_b0 = score(qb, 0, 512, "b0")
+        bank_b1 = score(qb, 512, 1024, "b1")
+
+        def part(j, lo, hi):
+            return lists[j][:, lo // 16 : hi // 16]
+
+        own = [keep.tile([P, HALF_I], F32, name=f"own{h}") for h in range(2)]
+        nc.vector.tensor_copy(own[0][:], a[:].indirect(part(0, 0, HALF_I)))
+        nc.scalar.activation(own[1][:], a[:].indirect(part(0, HALF_I, I)), ACT.Copy)
+        nc.scalar.copy(b[:, 0:512], bank_b0[:])
+        nc.scalar.copy(b[:, 512:1024], bank_b1[:])
+
+        x = keep.tile([P, I], F32, name="x")
+        y = keep.tile([P, I], F32, name="y")
+        ex = keep.tile([P, I], F32, name="ex")
+        ey = keep.tile([P, I], F32, name="ey")
+        for h in range(2):
+            lo, hi = h * HALF_I, (h + 1) * HALF_I
+            nc.vector.tensor_tensor(x[:, lo:hi], a[:].indirect(part(1, lo, hi)), own[h][:], ALU.subtract)
+        nc.scalar.activation(ex[:], x[:], ACT.Exp)
+        for h in range(2):
+            lo, hi = h * HALF_I, (h + 1) * HALF_I
+            nc.vector.tensor_tensor(y[:, lo:hi], b[:].indirect(part(2, lo, hi)), own[h][:], ALU.subtract)
+            nc.scalar.activation(ey[:, lo:hi], y[:, lo:hi], ACT.Exp)
+
+        lam_row = keep.tile([P, PIECE], F32, name="lam_row")
+        nc.gpsimd.tensor_copy(lam_row[:], lam_col[:].to_broadcast([P, PIECE]))
+
+        s = keep.tile([P, I], F32, name="s")
+        r = keep.tile([P, I], F32, name="r")
+        root = keep.tile([P, I - PIECE], F32, name="root")
+        nc.vector.scalar_tensor_tensor(s[:, :PIECE], ex[:, :PIECE], 1.0, ey[:, :PIECE], ALU.add, ALU.add)
+        nc.vector.reciprocal(r[:, :PIECE], s[:, :PIECE])
+        nc.vector.scalar_tensor_tensor(s[:, PIECE:], ex[:, PIECE:], 1.0, ey[:, PIECE:], ALU.add, ALU.add)
+        for lo in range(0, I, PIECE):
+            hi = lo + PIECE
+            if lo > 0:
+                nc.scalar.activation(root[:, lo - PIECE : hi - PIECE], s[:, lo:hi], ACT.Abs_reciprocal_sqrt)
+                nc.scalar.activation(r[:, lo:hi], root[:, lo - PIECE : hi - PIECE], ACT.Square)
+            nc.vector.tensor_tensor(placed[:].indirect(part(3, lo, hi)), r[:, lo:hi], lam_row[:], ALU.mult)
+
+        for n, lo in enumerate(range(0, T, STORE)):
+            res = keep.tile([P, STORE], F32, name=f"res{n}")
+            nc.vector.tensor_tensor(res[:], placed[:, lo : lo + STORE], old_sb[:, lo : lo + STORE], ALU.add)
+            queue = nc.sync if n % 2 == 0 else nc.scalar
+            queue.dma_start(out=out[:, lo : lo + STORE], in_=res[:])

@@ -31,20 +31,20 @@ def tile_attend_quotaratio_lean_putold_heads_kernel(
         keep = ctx.enter_context(tc.tile_pool(name="keep", bufs=1))
         psum = ctx.enter_context(tc.psum_pool(name="psum", bufs=1))
 
-        key_scale = keep.tile([P, T], U8, name="key_scale", align_bytes=64)
-        nc.vector.memset(key_scale[:].bitcast(I32), 0)
-        for g in range(4):
-            nc.scalar.dma_start(
-                out=key_scale[32 * g : 32 * g + 4, :].bitcast(I32),
-                in_=keys_scales[0, 4 * g : 4 * g + 4, :].bitcast(I32),
-            )
-
+        key_scale = keep.tile([P, 256], U8, name="key_scale", align_bytes=64)
+        nc.gpsimd.memset(key_scale[:].bitcast(I32), 0)
         words = keys_words[0].rearrange("p n t -> p (n t)").bitcast(I32)
         q_raw = [keep.tile([P, PACK, Q], F32, name=f"q_raw{j}") for j in range(2)]
-        key_code = [keep.tile([P, HALF_T], U32, name=f"key_code{h}", align_bytes=64) for h in range(2)]
-        for j, src in enumerate((query, query2)):
-            nc.sync.dma_start(out=q_raw[j][:], in_=src.rearrange("(p t) q -> p t q", t=PACK))
-            nc.sync.dma_start(out=key_code[j][:].bitcast(I32), in_=words[:, j * HALF_T : (j + 1) * HALF_T])
+        key_code = keep.tile([P, T], U32, name="key_code", align_bytes=64)
+        nc.sync.dma_start(out=q_raw[0][:], in_=query.rearrange("(p t) q -> p t q", t=PACK))
+        for g in range(4):
+            nc.sync.dma_start(
+                out=key_scale[32 * g : 32 * g + 16, :].bitcast(I32),
+                in_=keys_scales[0, 4 * g : 4 * g + 4, :].bitcast(I32).rearrange("r (j c) -> j r c", j=4),
+            )
+        nc.sync.dma_start(out=key_code[:, :768].bitcast(I32), in_=words[:, :768])
+        nc.sync.dma_start(out=q_raw[1][:], in_=query2.rearrange("(p t) q -> p t q", t=PACK))
+        nc.sync.dma_start(out=key_code[:, 768:].bitcast(I32), in_=words[:, 768:])
         lists = []
         for j, src in enumerate((offs, offs2, offs3, offs4)):
             tile = keep.tile([P, I // 16], U16, name=f"list{j}")
@@ -56,11 +56,16 @@ def tile_attend_quotaratio_lean_putold_heads_kernel(
         nc.sync.dma_start(out=old_sb[:], in_=old)
 
         placed = keep.tile([P, T], F32, name="placed")
-        nc.vector.memset(placed[:], 0.0)
+        nc.gpsimd.memset(placed[:], 0.0)
 
         def quantise(j):
             grouped = keep.tile([P, Q, PACK], BF16, name=f"grouped{j}", align_bytes=64)
-            nc.vector.tensor_copy(out=grouped[:], in_=q_raw[j][:].rearrange("p t q -> p q t"))
+            turned = q_raw[j][:].rearrange("p t q -> p q t")
+            if j == 0:
+                nc.vector.tensor_copy(out=grouped[:, :80, :], in_=turned[:, :80, :])
+                nc.scalar.copy(grouped[:, 80:, :], turned[:, 80:, :])
+            else:
+                nc.vector.tensor_copy(out=grouped[:], in_=turned)
             code = keep.tile([P, Q], U32, name=f"q_code{j}", align_bytes=64)
             scale = keep.tile([P, Q], U8, name=f"q_scale{j}", align_bytes=64)
             nc.vector.quantize_mx(
@@ -69,35 +74,40 @@ def tile_attend_quotaratio_lean_putold_heads_kernel(
             return code, scale
 
         def score(qq, lo, hi, name):
-            bank = psum.tile([P, hi - lo], F32, name=name)
-            h = lo // HALF_T
-            nc.tensor.matmul_mx(
-                out=bank[:],
-                lhsT=qq[0][:].bitcast(FP8X4),
-                lhsT_scale=qq[1][:],
-                rhs=key_code[h][:, lo - h * HALF_T : hi - h * HALF_T].bitcast(FP8X4),
-                rhs_scale=key_scale[:, lo:hi],
-                start=True,
-                stop=True,
-            )
+            bank = psum.tile([P, hi - lo], F32, name=name, tag=name)
+            for c0 in range(lo, hi, 256):
+                c1 = min(hi, c0 + 256)
+                j = c0 // 256
+                nc.tensor.matmul_mx(
+                    out=bank[:, c0 - lo : c1 - lo],
+                    lhsT=qq[0][:].bitcast(FP8X4),
+                    lhsT_scale=qq[1][:],
+                    rhs=key_code[:, c0:c1].bitcast(FP8X4),
+                    rhs_scale=key_scale[4 * j :, c0 - 256 * j : c1 - 256 * j],
+                    start=True,
+                    stop=True,
+                )
             return bank
 
         a = keep.tile([P, T], F32, name="a")
         b = keep.tile([P, T], F32, name="b")
         qa = quantise(0)
-        nc.scalar.copy(a[:, 0:512], score(qa, 0, 512, "a0")[:])
         qb = quantise(1)
-        nc.scalar.copy(a[:, 512:768], score(qa, 512, 768, "a1")[:])
-        nc.vector.tensor_copy(a[:, 768:1024], score(qa, 768, 1024, "a2")[:])
-        bank_b0 = score(qb, 0, 512, "b0")
-        bank_b1 = score(qb, 512, 1024, "b1")
+        for lo, hi in ((0, 256), (256, 512), (512, 768), (768, 896), (896, 1024)):
+            bank = score(qa, lo, hi, f"a{lo}")
+            if lo in (0, 768):
+                nc.vector.tensor_copy(a[:, lo:hi], bank[:])
+            else:
+                nc.scalar.copy(a[:, lo:hi], bank[:])
+        bank_b0 = score(qb, 0, 512, "a768")
+        bank_b1 = score(qb, 512, 1024, "a896")
 
         def part(j, lo, hi):
             return lists[j][:, lo // 16 : hi // 16]
 
-        own = [keep.tile([P, HALF_I], F32, name=f"own{h}") for h in range(2)]
-        nc.vector.tensor_copy(own[0][:], a[:].indirect(part(0, 0, HALF_I)))
-        nc.scalar.activation(own[1][:], a[:].indirect(part(0, HALF_I, I)), ACT.Copy)
+        own = keep.tile([P, I], F32, name="own")
+        nc.vector.tensor_copy(own[:, :HALF_I], a[:].indirect(part(0, 0, HALF_I)))
+        nc.scalar.activation(own[:, HALF_I:], a[:].indirect(part(0, HALF_I, I)), ACT.Copy)
         nc.scalar.copy(b[:, 0:512], bank_b0[:])
         nc.scalar.copy(b[:, 512:1024], bank_b1[:])
 
@@ -105,30 +115,35 @@ def tile_attend_quotaratio_lean_putold_heads_kernel(
         y = keep.tile([P, I], F32, name="y")
         ex = keep.tile([P, I], F32, name="ex")
         ey = keep.tile([P, I], F32, name="ey")
-        for h in range(2):
-            lo, hi = h * HALF_I, (h + 1) * HALF_I
-            nc.vector.tensor_tensor(x[:, lo:hi], a[:].indirect(part(1, lo, hi)), own[h][:], ALU.subtract)
+        nc.vector.tensor_tensor(x[:], a[:].indirect(lists[1][:]), own[:], ALU.subtract)
         nc.scalar.activation(ex[:], x[:], ACT.Exp)
-        for h in range(2):
-            lo, hi = h * HALF_I, (h + 1) * HALF_I
-            nc.vector.tensor_tensor(y[:, lo:hi], b[:].indirect(part(2, lo, hi)), own[h][:], ALU.subtract)
+        for lo in (0, HALF_I):
+            hi = lo + HALF_I
+            nc.vector.tensor_tensor(y[:, lo:hi], b[:].indirect(part(2, lo, hi)), own[:, lo:hi], ALU.subtract)
             nc.scalar.activation(ey[:, lo:hi], y[:, lo:hi], ACT.Exp)
 
         lam_row = keep.tile([P, PIECE], F32, name="lam_row")
-        nc.gpsimd.tensor_copy(lam_row[:], lam_col[:].to_broadcast([P, PIECE]))
-
+        nc.vector.tensor_copy(lam_row[:], lam_col[:].to_broadcast([P, PIECE]))
+        rest = I - PIECE
         s = keep.tile([P, I], F32, name="s")
-        r = keep.tile([P, I], F32, name="r")
-        root = keep.tile([P, I - PIECE], F32, name="root")
-        nc.vector.scalar_tensor_tensor(s[:, :PIECE], ex[:, :PIECE], 1.0, ey[:, :PIECE], ALU.add, ALU.add)
-        nc.vector.reciprocal(r[:, :PIECE], s[:, :PIECE])
-        nc.vector.scalar_tensor_tensor(s[:, PIECE:], ex[:, PIECE:], 1.0, ey[:, PIECE:], ALU.add, ALU.add)
-        for lo in range(0, I, PIECE):
-            hi = lo + PIECE
-            if lo > 0:
-                nc.scalar.activation(root[:, lo - PIECE : hi - PIECE], s[:, lo:hi], ACT.Abs_reciprocal_sqrt)
-                nc.scalar.activation(r[:, lo:hi], root[:, lo - PIECE : hi - PIECE], ACT.Square)
-            nc.vector.tensor_tensor(placed[:].indirect(part(3, lo, hi)), r[:, lo:hi], lam_row[:], ALU.mult)
+        r = keep.tile([P, PIECE], F32, name="r")
+        root = keep.tile([P, rest], F32, name="root")
+        root_lam = keep.tile([P, rest], F32, name="root_lam")
+
+        def denominator(lo, hi):
+            nc.vector.scalar_tensor_tensor(s[:, lo:hi], ex[:, lo:hi], 1.0, ey[:, lo:hi], ALU.add, ALU.add)
+
+        denominator(0, PIECE)
+        denominator(PIECE, HALF_I)
+        nc.vector.reciprocal(r[:], s[:, :PIECE])
+        denominator(HALF_I, I)
+        nc.vector.tensor_tensor(placed[:].indirect(part(3, 0, PIECE)), r[:], lam_row[:], ALU.mult)
+        halves = ((0, rest // 2), (rest // 2, rest))
+        for lo, hi in halves:
+            nc.scalar.activation(root[:, lo:hi], s[:, PIECE + lo : PIECE + hi], ACT.Abs_reciprocal_sqrt)
+        for lo, hi in halves:
+            nc.scalar.activation(root_lam[:, lo:hi], root[:, lo:hi], ACT.Copy, scale=lam_col[:])
+        nc.vector.tensor_tensor(placed[:].indirect(part(3, PIECE, I)), root[:], root_lam[:], ALU.mult)
 
         for n, lo in enumerate(range(0, T, STORE)):
             res = keep.tile([P, STORE], F32, name=f"res{n}")

from contextlib import ExitStack

import concourse.mybir as mybir

D, T, I, Q = 512, 1024, 512, 128
FLOPS = 2 * 2 * D * T * Q

F32 = mybir.dt.float32
BF16 = mybir.dt.bfloat16
I32 = mybir.dt.int32
U32 = mybir.dt.uint32
U16 = mybir.dt.uint16
U8 = mybir.dt.uint8
FP8X4 = mybir.dt.float8_e4m3fn_x4
ALU = mybir.AluOpType
ACT = mybir.ActivationFunctionType

P = 128
PACK = 4
HALF_T = T // 2
HALF_I = I // 2
PIECE = 128
STORE = 256


def tile_attend_quotaratio_lean_putold_heads_kernel(
    tc, query, query2, keys_words, keys_scales, lam, old, offs, offs2, offs3, offs4, out
):
    nc = tc.nc
    with ExitStack() as ctx:
        keep = ctx.enter_context(tc.tile_pool(name="keep", bufs=1))
        psum = ctx.enter_context(tc.psum_pool(name="psum", bufs=1))

        key_scale = keep.tile([P, 256], U8, name="key_scale", align_bytes=64)
        nc.gpsimd.memset(key_scale[:].bitcast(I32), 0)
        words = keys_words[0].rearrange("p n t -> p (n t)").bitcast(I32)
        q_raw = [keep.tile([P, PACK, Q], F32, name=f"q_raw{j}") for j in range(2)]
        key_code = keep.tile([P, T], U32, name="key_code", align_bytes=64)
        nc.sync.dma_start(out=q_raw[0][:], in_=query.rearrange("(p t) q -> p t q", t=PACK))
        for g in range(4):
            nc.sync.dma_start(
                out=key_scale[32 * g : 32 * g + 16, :].bitcast(I32),
                in_=keys_scales[0, 4 * g : 4 * g + 4, :].bitcast(I32).rearrange("r (j c) -> j r c", j=4),
            )
        nc.sync.dma_start(out=key_code[:, :768].bitcast(I32), in_=words[:, :768])
        nc.sync.dma_start(out=q_raw[1][:], in_=query2.rearrange("(p t) q -> p t q", t=PACK))
        nc.sync.dma_start(out=key_code[:, 768:].bitcast(I32), in_=words[:, 768:])
        lists = []
        for j, src in enumerate((offs, offs2, offs3, offs4)):
            tile = keep.tile([P, I // 16], U16, name=f"list{j}")
            nc.sync.dma_start(tile[:], src)
            lists.append(tile)
        lam_col = keep.tile([P, 1], F32, name="lam_col")
        nc.sync.dma_start(out=lam_col[:], in_=lam)
        old_sb = keep.tile([P, T], F32, name="old_sb")
        nc.sync.dma_start(out=old_sb[:], in_=old)

        placed = keep.tile([P, T], F32, name="placed")
        nc.gpsimd.memset(placed[:], 0.0)

        def quantise(j):
            grouped = keep.tile([P, Q, PACK], BF16, name=f"grouped{j}", align_bytes=64)
            turned = q_raw[j][:].rearrange("p t q -> p q t")
            if j == 0:
                nc.vector.tensor_copy(out=grouped[:, :80, :], in_=turned[:, :80, :])
                nc.scalar.copy(grouped[:, 80:, :], turned[:, 80:, :])
            else:
                nc.vector.tensor_copy(out=grouped[:], in_=turned)
            code = keep.tile([P, Q], U32, name=f"q_code{j}", align_bytes=64)
            scale = keep.tile([P, Q], U8, name=f"q_scale{j}", align_bytes=64)
            nc.vector.quantize_mx(
                out=code[:].bitcast(FP8X4), scales=scale[:], in_=grouped[:].rearrange("p q t -> p (q t)")
            )
            return code, scale

        def score(qq, lo, hi, name):
            bank = psum.tile([P, hi - lo], F32, name=name, tag=name)
            for c0 in range(lo, hi, 256):
                c1 = min(hi, c0 + 256)
                j = c0 // 256
                nc.tensor.matmul_mx(
                    out=bank[:, c0 - lo : c1 - lo],
                    lhsT=qq[0][:].bitcast(FP8X4),
                    lhsT_scale=qq[1][:],
                    rhs=key_code[:, c0:c1].bitcast(FP8X4),
                    rhs_scale=key_scale[4 * j :, c0 - 256 * j : c1 - 256 * j],
                    start=True,
                    stop=True,
                )
            return bank

        a = keep.tile([P, T], F32, name="a")
        b = keep.tile([P, T], F32, name="b")
        qa = quantise(0)
        qb = quantise(1)
        for lo, hi in ((0, 256), (256, 512), (512, 768), (768, 896), (896, 1024)):
            bank = score(qa, lo, hi, f"a{lo}")
            if lo in (0, 768):
                nc.vector.tensor_copy(a[:, lo:hi], bank[:])
            else:
                nc.scalar.copy(a[:, lo:hi], bank[:])
        bank_b0 = score(qb, 0, 512, "a768")
        bank_b1 = score(qb, 512, 1024, "a896")

        def part(j, lo, hi):
            return lists[j][:, lo // 16 : hi // 16]

        own = keep.tile([P, I], F32, name="own")
        nc.vector.tensor_copy(own[:, :HALF_I], a[:].indirect(part(0, 0, HALF_I)))
        nc.scalar.activation(own[:, HALF_I:], a[:].indirect(part(0, HALF_I, I)), ACT.Copy)
        nc.scalar.copy(b[:, 0:512], bank_b0[:])
        nc.scalar.copy(b[:, 512:1024], bank_b1[:])

        x = keep.tile([P, I], F32, name="x")
        y = keep.tile([P, I], F32, name="y")
        ex = keep.tile([P, I], F32, name="ex")
        ey = keep.tile([P, I], F32, name="ey")
        nc.vector.tensor_tensor(x[:], a[:].indirect(lists[1][:]), own[:], ALU.subtract)
        nc.scalar.activation(ex[:], x[:], ACT.Exp)
        for lo in (0, HALF_I):
            hi = lo + HALF_I
            nc.vector.tensor_tensor(y[:, lo:hi], b[:].indirect(part(2, lo, hi)), own[:, lo:hi], ALU.subtract)
            nc.scalar.activation(ey[:, lo:hi], y[:, lo:hi], ACT.Exp)

        lam_row = keep.tile([P, PIECE], F32, name="lam_row")
        nc.vector.tensor_copy(lam_row[:], lam_col[:].to_broadcast([P, PIECE]))
        rest = I - PIECE
        s = keep.tile([P, I], F32, name="s")
        r = keep.tile([P, PIECE], F32, name="r")
        root = keep.tile([P, rest], F32, name="root")
        root_lam = keep.tile([P, rest], F32, name="root_lam")

        def denominator(lo, hi):
            nc.vector.scalar_tensor_tensor(s[:, lo:hi], ex[:, lo:hi], 1.0, ey[:, lo:hi], ALU.add, ALU.add)

        denominator(0, PIECE)
        denominator(PIECE, HALF_I)
        nc.vector.reciprocal(r[:], s[:, :PIECE])
        denominator(HALF_I, I)
        nc.vector.tensor_tensor(placed[:].indirect(part(3, 0, PIECE)), r[:], lam_row[:], ALU.mult)
        halves = ((0, rest // 2), (rest // 2, rest))
        for lo, hi in halves:
            nc.scalar.activation(root[:, lo:hi], s[:, PIECE + lo : PIECE + hi], ACT.Abs_reciprocal_sqrt)
        for lo, hi in halves:
            nc.scalar.activation(root_lam[:, lo:hi], root[:, lo:hi], ACT.Copy, scale=lam_col[:])
        nc.vector.tensor_tensor(placed[:].indirect(part(3, PIECE, I)), root[:], root_lam[:], ALU.mult)

        for n, lo in enumerate(range(0, T, STORE)):
            res = keep.tile([P, STORE], F32, name=f"res{n}")
            nc.vector.tensor_tensor(res[:], placed[:, lo : lo + STORE], old_sb[:, lo : lo + STORE], ALU.add)
            queue = nc.sync if n % 2 == 0 else nc.scalar
            queue.dma_start(out=out[:, lo : lo + STORE], in_=res[:])
